import numpy as np
import ml_dtypes


def mxq(x, axis, fmt="e4m3"):
    dtype, down = {"e4m3": (ml_dtypes.float8_e4m3fn, 7), "e5m2": (ml_dtypes.float8_e5m2, 14)}[fmt]
    v = np.moveaxis(np.asarray(x, np.float32).astype(ml_dtypes.bfloat16).astype(np.float64), axis, -1)
    blocks = v.reshape(v.shape[:-1] + (-1, 32))
    amax = np.abs(blocks).max(-1, keepdims=True)
    byte = np.maximum(np.where(amax > 0, np.frexp(amax)[1] - 1 + 127, 0) - down, 1)
    scale = np.exp2(byte - 127.0)
    codes = (blocks / scale).astype(np.float32).astype(dtype).astype(np.float64)
    return np.moveaxis((codes * scale).reshape(v.shape), -1, axis)


WIDE = False


def mx_kscale(k):
    if not WIDE:
        return np.ones(k)
    levels = np.array([10, -10, 5, -5, 0])
    if k % 512:
        return np.exp2(np.random.permutation(np.resize(levels, k // 32))).repeat(32)
    a = np.empty((k // 512, 16))
    for p in range(k // 512):
        a[p, :8] = np.random.permutation(np.resize(levels, 8))
        for g in range(8):
            far = levels[np.abs(levels - a[p, g]) >= 10]
            a[p, g + 8] = far[np.random.randint(len(far))]
    return np.exp2(a.ravel()).repeat(32)


def f64(x):
    return np.asarray(x).astype(np.float64)


def striped8(idx):
    return np.asarray(idx).reshape(8, -1, 16).transpose(0, 2, 1).reshape(128, -1).astype(np.uint16)


def unstriped8(offs):
    return offs.reshape(8, 16, -1).transpose(0, 2, 1).reshape(8, -1).astype(np.int64)


def pick8(x, idx, run):
    r = np.arange(len(x))
    return x[r[:, None], idx[r % (8 * run) // run]]


E2M1 = np.array([0.0, 0.5, 1.0, 1.5, 2.0, 3.0, 4.0, 6.0, -0.0, -0.5, -1.0, -1.5, -2.0, -3.0, -4.0, -6.0])


def pack_weight(w, fmt):
    k, n = w.shape
    w = f64(np.asarray(w, np.float32).astype(ml_dtypes.bfloat16)).reshape(k // 32, 32, n)
    amax = np.abs(w).max(1)
    if fmt == "e4m3":
        byte = np.frexp(amax)[1] - 1 + 127 - 7
    else:
        mant, ex = np.frexp(amax / 6.0)
        byte = np.where(mant > 0.5, ex, ex - 1) + 127
    byte = np.clip(np.where(amax > 0, byte, 1), 1, 254)
    scaled = (w * np.exp2(127.0 - byte)[:, None, :]).reshape(k, n).astype(np.float32)
    by_word = np.ascontiguousarray(scaled.reshape(k // 512, 128, 4, n).transpose(0, 1, 3, 2))
    if fmt == "e4m3":
        words = by_word.astype(ml_dtypes.float8_e4m3fn).view(np.uint8)
    else:
        c = by_word.astype(ml_dtypes.float4_e2m1fn).view(np.uint8) & 0xF
        words = (c[..., 0::2] | (c[..., 1::2] << 4)).reshape(k // 512, 128, 2 * n)
    return np.ascontiguousarray(words), np.ascontiguousarray(byte.astype(np.uint8).reshape(k // 512, 16, n))


def unpack_weight(words, scales, fmt):
    g, _, n = scales.shape
    words = np.ascontiguousarray(words).reshape(g, 128, n, -1)
    if fmt == "e4m3":
        vals = words.view(ml_dtypes.float8_e4m3fn).astype(np.float64)
    else:
        nib = np.empty((g, 128, n, 4), np.uint8)
        nib[..., 0::2] = words & 0xF
        nib[..., 1::2] = words >> 4
        vals = E2M1[nib]
    vals = vals * np.repeat(np.exp2(scales.astype(np.float64) - 127.0), 8, axis=1)[..., None]
    return vals.transpose(0, 1, 3, 2).reshape(g * 512, n)


D, T, U, X, I, Q, E = 512, 1024, 1024, 1024, 512, 512, 256


def setup_inputs():
    n = np.random.standard_normal
    idx = np.stack([np.random.permutation(T)[:I] for _ in range(8)])
    idx2 = np.stack([np.random.permutation(U)[:I] for _ in range(8)])
    idx3 = np.stack([np.random.permutation(U)[:I] for _ in range(8)])
    idx4 = np.stack([np.random.permutation(X)[:I] for _ in range(8)])
    idx5 = np.stack([np.random.permutation(X)[:I] for _ in range(8)])
    fd = mx_kscale(D)
    fq = mx_kscale(Q)
    keysp = pack_weight(n((D, T)) / fd[:, None], "e4m3")
    notesp = pack_weight(n((D, U)) / fd[:, None], "e2m1")
    usersp = pack_weight(n((D, X)) / fd[:, None], "e2m1")
    mixp = pack_weight(n((Q, E)) * 1.0 / np.sqrt(Q) / fq[:, None], "e2m1")
    return {
        "query": (n((D, Q)) * 1.0 / np.sqrt(D) * fd[:, None]).astype(np.float32),
        "query2": (n((D, Q)) * 1.0 / np.sqrt(D) * fd[:, None]).astype(np.float32),
        "keys_words": keysp[0],
        "keys_scales": keysp[1],
        "notes_words": notesp[0],
        "notes_scales": notesp[1],
        "users_words": usersp[0],
        "users_scales": usersp[1],
        "rowf": (np.random.uniform(0.5, 2.0, (Q, 1)) * fq[:, None]).astype(np.float32),
        "mix_words": mixp[0],
        "mix_scales": mixp[1],
        "offs": striped8(idx),
        "offs2": striped8(idx2),
        "offs3": striped8(idx3),
        "offs4": striped8(idx4),
        "offs5": striped8(idx5),
    }


def reference(query, query2, keys_words, keys_scales, notes_words, notes_scales, users_words, users_scales, rowf, mix_words, mix_scales, offs, offs2, offs3, offs4, offs5):
    idx = unstriped8(offs)
    idx2 = unstriped8(offs2)
    idx3 = unstriped8(offs3)
    idx4 = unstriped8(offs4)
    idx5 = unstriped8(offs5)
    keysu = unpack_weight(keys_words, keys_scales, "e4m3")
    notesu = unpack_weight(notes_words, notes_scales, "e2m1")
    usersu = unpack_weight(users_words, users_scales, "e2m1")
    mixu = unpack_weight(mix_words, mix_scales, "e2m1")
    queryq = mxq(f64(query), 0, "e4m3")
    a = queryq.T @ keysu
    b = queryq.T @ notesu
    query2q = mxq(f64(query2), 0, "e4m3")
    c0 = query2q.T @ usersu
    f1 = np.zeros((Q, U))
    f1[np.arange(Q)[:, None], idx2[np.arange(Q) % 512 // 64]] = pick8(a, idx, 64)
    cc = b + f1
    f2 = np.zeros((Q, X))
    f2[np.arange(Q)[:, None], idx4[np.arange(Q) % 512 // 64]] = pick8(cc, idx3, 64)
    dd = c0 + f2
    g = pick8(dd, idx5, 64)
    gw = g * f64(rowf)
    gwq = mxq(gw, 0, "e4m3")
    y = mixu.T @ gwq
    return y

@@ -1,0 +1,212 @@
+from contextlib import ExitStack
+
+import concourse.mybir as mybir
+
+D, COLS, SLOTS, Q, E = 512, 1024, 512, 512, 256
+FLOPS = 2 * D * Q * COLS * 3 + 2 * Q * E * SLOTS
+
+F32 = mybir.dt.float32
+BF16 = mybir.dt.bfloat16
+I32 = mybir.dt.int32
+U32 = mybir.dt.uint32
+U16 = mybir.dt.uint16
+U8 = mybir.dt.uint8
+FP8X4 = mybir.dt.float8_e4m3fn_x4
+FP4X4 = mybir.dt.float4_e2m1fn_x4
+ADD = mybir.AluOpType.add
+MULT = mybir.AluOpType.mult
+COPY = mybir.ActivationFunctionType.Copy
+
+P = 128
+PACK = 4
+BANK = 512
+WINDOWS = 3
+LIST_COLS = SLOTS // 16
+
+
+def tile_attend_relaythree_threeq_mixed_kernel(
+    tc, query, query2, keys_words, keys_scales, notes_words, notes_scales, users_words, users_scales,
+    rowf, mix_words, mix_scales, offs, offs2, offs3, offs4, offs5, out,
+):
+    nc = tc.nc
+    with ExitStack() as ctx:
+        keep = ctx.enter_context(tc.tile_pool(name="keep", bufs=1))
+        psum = ctx.enter_context(tc.psum_pool(name="psum", bufs=1))
+        ring = [[psum.tile([P, BANK], F32, name=f"ring{s}_{h}") for h in range(2)] for s in range(2)]
+
+        def load_list(name, source):
+            tile = keep.tile([P, LIST_COLS], U16, name=name)
+            nc.sync.dma_start(tile[:], source)
+            return tile
+
+        def load_query(name, source):
+            halves = []
+            for h in range(2):
+                raw = keep.tile([P, PACK, Q // 2], F32, name=f"{name}_raw{h}", tag=f"{name}_raw{h}")
+                nc.sync.dma_start(
+                    out=raw[:],
+                    in_=source.rearrange("(p t) q -> p t q", t=PACK)[:, :, h * (Q // 2) : (h + 1) * (Q // 2)],
+                )
+                halves.append(raw)
+            return halves
+
+        def load_words(name, source):
+            tile = keep.tile([P, source.shape[1]], U8, name=name, align_bytes=64)
+            nc.sync.dma_start(out=tile[:].bitcast(I32), in_=source.bitcast(I32))
+            return tile
+
+        def load_scales(name, source, queue):
+            tile = keep.tile([P, source.shape[2]], U8, name=name, align_bytes=64)
+            for j in range(4):
+                queue.dma_start(out=tile[j:P:32, :].bitcast(I32), in_=source[0, j:16:4, :].bitcast(I32))
+            return tile
+
+        q_raw = load_query("q", query)
+        keys_s = load_scales("keys_s", keys_scales, nc.scalar)
+        keys_w = load_words("keys_w", keys_words[0].rearrange("p n t -> p (n t)"))
+        list1 = load_list("list1", offs)
+        list2 = load_list("list2", offs2)
+        notes_w = load_words("notes_w", notes_words[0])
+        notes_s = load_scales("notes_s", notes_scales, nc.sync)
+        q2_raw = load_query("q2", query2)
+        list3 = load_list("list3", offs3)
+        list4 = load_list("list4", offs4)
+        users_w = load_words("users_w", users_words[0])
+        users_s = load_scales("users_s", users_scales, nc.sync)
+        list5 = load_list("list5", offs5)
+        row_factor = keep.tile([P, PACK], F32)
+        nc.sync.dma_start(out=row_factor[:], in_=rowf.rearrange("(p t) o -> p (t o)", t=PACK))
+        mix_w = load_words("mix_w", mix_words[0])
+        mix_s = load_scales("mix_s", mix_scales, nc.sync)
+
+        f1 = [keep.tile([P, COLS], F32, name=f"f1_{w}") for w in range(WINDOWS)]
+        f2 = [keep.tile([P, COLS], F32, name="f2_0")]
+        for window in f1 + f2:
+            nc.vector.memset(window[:], 0.0)
+
+        def round_query(name, halves, copy):
+            dealt = keep.tile([P, PACK, P, PACK], BF16, name=f"{name}_dealt", align_bytes=64)
+            for h, raw in enumerate(halves):
+                copy(
+                    out=dealt[:, :, h * (P // 2) : (h + 1) * (P // 2), :].rearrange("p r s t -> p s r t"),
+                    in_=raw[:].rearrange("p t (s r) -> p s r t", r=PACK),
+                )
+            return dealt
+
+        def quantize(name, values):
+            width = values.shape[1] // PACK
+            codes = keep.tile([P, width], U32, name=f"{name}_codes", align_bytes=64)
+            scales = keep.tile([P, width], U8, name=f"{name}_scales", align_bytes=64)
+            nc.vector.quantize_mx(out=codes[:].bitcast(FP8X4), scales=scales[:], in_=values)
+            return codes, scales
+
+        def scores(banks, stationary, words, scales, dtype, word_bytes):
+            codes, code_scales = stationary
+            for half, bank in enumerate(banks):
+                nc.tensor.matmul_mx(
+                    out=bank[:],
+                    lhsT=codes.bitcast(FP8X4),
+                    lhsT_scale=code_scales,
+                    rhs=words[:, half * BANK * word_bytes : (half + 1) * BANK * word_bytes].bitcast(dtype),
+                    rhs_scale=scales[:, half * BANK : (half + 1) * BANK],
+                    start=True,
+                    stop=True,
+                )
+
+        q_dealt = round_query("q", q_raw, nc.vector.tensor_copy)
+        q_first = quantize("q_first", q_dealt[:, 0, :, :].rearrange("p s t -> p (s t)"))
+        q_rest = quantize("q_rest", q_dealt[:, 1:, :, :].rearrange("p r s t -> p (r s t)"))
+        q_tiles = [(q_first[0][:], q_first[1][:])] + [
+            (q_rest[0][:, r * P : (r + 1) * P], q_rest[1][:, r * P : (r + 1) * P]) for r in range(PACK - 1)
+        ]
+
+        for h in range(2):
+            window = keep.tile([P, COLS], F32, name=f"f2_{h + 1}", tag=f"q_raw{h}")
+            nc.vector.memset(window[:], 0.0)
+            f2.append(window)
+
+        def pick_and_place_a(r):
+            a = keep.tile([P, COLS], F32, name=f"a{r}")
+            scores(ring[r % 2], q_tiles[r], keys_w, keys_s, FP8X4, 4)
+            for half, bank in enumerate(ring[r % 2]):
+                copy = nc.vector.tensor_copy if (r == 0 and half == 1) else nc.scalar.copy
+                copy(out=a[:, half * BANK : (half + 1) * BANK], in_=bank[:])
+            pieces = 2 if r == 0 else 1
+            picked = []
+            for piece in range(pieces):
+                cols = slice(piece * LIST_COLS // pieces, (piece + 1) * LIST_COLS // pieces)
+                values = keep.tile([P, SLOTS // pieces], F32, name=f"a_picked{r}_{piece}")
+                nc.scalar.activation(values[:], a[:].indirect(list1[:, cols]), COPY)
+                picked.append((cols, values))
+            return picked
+
+        def place(window, places, picked):
+            for cols, values in picked:
+                nc.vector.tensor_copy(window[:].indirect(places[:, cols]), values[:])
+
+        def add_scores(name, banks, window):
+            total = keep.tile([P, COLS], F32, name=name)
+            for half, bank in enumerate(banks):
+                cols = slice(half * BANK, (half + 1) * BANK)
+                nc.vector.tensor_tensor(total[:, cols], bank[:], window[:, cols], ADD)
+            return total
+
+        a_picked = [pick_and_place_a(r) for r in range(PACK)]
+        q2_dealt = round_query("q2", q2_raw, nc.scalar.copy)
+        cc = []
+        place(f1[0], list2, a_picked[0])
+        for r in range(PACK):
+            if r + 1 < PACK:
+                place(f1[(r + 1) % WINDOWS], list2, a_picked[r + 1])
+            scores(ring[r % 2], q_tiles[r], notes_w, notes_s, FP4X4, 2)
+            cc.append(add_scores(f"cc{r}", ring[r % 2], f1[r % WINDOWS]))
+
+        q2_codes, q2_scales = quantize("q2", q2_dealt[:].rearrange("p r s t -> p (r s t)"))
+        cc_picked = []
+        for r in range(PACK):
+            values = keep.tile([P, SLOTS], F32, name=f"cc_picked{r}")
+            nc.scalar.activation(values[:], cc[r][:].indirect(list3[:]), COPY)
+            cc_picked.append([(slice(0, LIST_COLS), values)])
+
+        half_slots = SLOTS // 2
+        gw = [keep.tile([P, half_slots, PACK], BF16, name=f"gw{h}", align_bytes=64) for h in range(2)]
+        place(f2[0], list4, cc_picked[0])
+        for r in range(PACK):
+            if r + 1 < PACK:
+                place(f2[(r + 1) % WINDOWS], list4, cc_picked[r + 1])
+            cols = slice(r * P, (r + 1) * P)
+            scores(ring[r % 2], (q2_codes[:, cols], q2_scales[:, cols]), users_w, users_s, FP4X4, 2)
+            dd = add_scores(f"dd{r}", ring[r % 2], f2[r % WINDOWS])
+            factor = row_factor[:, r : r + 1]
+            for h in range(2):
+                g = keep.tile([P, half_slots], F32, name=f"g{r}_{h}")
+                window = dd[:].indirect(list5[:, h * LIST_COLS // 2 : (h + 1) * LIST_COLS // 2])
+                if r == PACK - 1 and h == 0:
+                    nc.vector.tensor_copy(g[:], window)
+                else:
+                    nc.scalar.activation(g[:], window, COPY)
+                if r < 2 or h == 1:
+                    nc.scalar.activation(gw[h][:, :, r], g[:], COPY, scale=factor)
+                else:
+                    nc.vector.tensor_scalar_mul(gw[h][:, :, r], g[:], factor)
+
+        for h in range(2):
+            codes, scales = quantize(f"gw{h}", gw[h][:].rearrange("p i r -> p (i r)"))
+            bank = psum.tile([P, 2, half_slots], F32, name=f"y{h}")
+            for e in range(2):
+                nc.tensor.matmul_mx(
+                    out=bank[:, e, :],
+                    lhsT=mix_w[:, e * 2 * P : (e + 1) * 2 * P].bitcast(FP4X4),
+                    lhsT_scale=mix_s[:, e * P : (e + 1) * P],
+                    rhs=codes[:].bitcast(FP8X4),
+                    rhs_scale=scales[:],
+                    start=True,
+                    stop=True,
+                )
+            y = keep.tile([P, 2, half_slots], F32, name=f"y_out{h}")
+            copy = nc.scalar.copy if h == 0 else nc.vector.tensor_copy
+            copy(out=y[:], in_=bank[:])
+            queue = nc.scalar if h == 0 else nc.sync
+            queue.dma_start(
+                out=out.rearrange("(e p) i -> p e i", p=P)[:, :, h * half_slots : (h + 1) * half_slots], in_=y[:]
+            )

@@ -32,7 +32,7 @@ def tile_attend_relaythree_threeq_mixed_kernel(
     with ExitStack() as ctx:
         keep = ctx.enter_context(tc.tile_pool(name="keep", bufs=1))
         psum = ctx.enter_context(tc.psum_pool(name="psum", bufs=1))
-        ring = [[psum.tile([P, BANK], F32, name=f"ring{s}_{h}") for h in range(2)] for s in range(2)]
+        ring = [[psum.tile([P, BANK], F32, name=f"ring{s}_{h}") for h in range(2)] for s in range(3)]
 
         def load_list(name, source):
             tile = keep.tile([P, LIST_COLS], U16, name=name)
@@ -125,66 +125,84 @@ def tile_attend_relaythree_threeq_mixed_kernel(
             nc.vector.memset(window[:], 0.0)
             f2.append(window)
 
-        def pick_and_place_a(r):
-            a = keep.tile([P, COLS], F32, name=f"a{r}")
-            scores(ring[r % 2], q_tiles[r], keys_w, keys_s, FP8X4, 4)
-            for half, bank in enumerate(ring[r % 2]):
-                copy = nc.vector.tensor_copy if (r == 0 and half == 1) else nc.scalar.copy
-                copy(out=a[:, half * BANK : (half + 1) * BANK], in_=bank[:])
-            pieces = 2 if r == 0 else 1
-            picked = []
-            for piece in range(pieces):
-                cols = slice(piece * LIST_COLS // pieces, (piece + 1) * LIST_COLS // pieces)
-                values = keep.tile([P, SLOTS // pieces], F32, name=f"a_picked{r}_{piece}")
-                nc.scalar.activation(values[:], a[:].indirect(list1[:, cols]), COPY)
-                picked.append((cols, values))
-            return picked
+        def pick(name, window, entries, cols):
+            values = keep.tile([P, 16 * (cols.stop - cols.start)], F32, name=name)
+            nc.scalar.activation(values[:], window[:].indirect(entries[:, cols]), COPY)
+            return values
 
-        def place(window, places, picked):
-            for cols, values in picked:
-                nc.vector.tensor_copy(window[:].indirect(places[:, cols]), values[:])
+        def place(window, places, cols, values):
+            nc.vector.tensor_copy(window[:].indirect(places[:, cols]), values[:])
 
-        def add_scores(name, banks, window):
+        def leave_psum(name, banks, second_copy):
+            whole = keep.tile([P, COLS], F32, name=name)
+            nc.scalar.copy(out=whole[:, :BANK], in_=banks[0][:])
+            second_copy(out=whole[:, BANK:], in_=banks[1][:])
+            return whole
+
+        def add_in_sbuf(name, banks, window):
+            total = keep.tile([P, COLS], F32, name=name)
+            nc.gpsimd.tensor_tensor(total[:], leave_psum(name + "_term", banks, nc.scalar.copy)[:], window[:], ADD)
+            return total
+
+        def add_from_psum(name, banks, window):
             total = keep.tile([P, COLS], F32, name=name)
             for half, bank in enumerate(banks):
                 cols = slice(half * BANK, (half + 1) * BANK)
                 nc.vector.tensor_tensor(total[:, cols], bank[:], window[:, cols], ADD)
             return total
 
-        a_picked = [pick_and_place_a(r) for r in range(PACK)]
-        q2_dealt = round_query("q2", q2_raw, nc.scalar.copy)
+        def round_on_gpsimd(out, in_):
+            nc.gpsimd.tensor_scalar(out, in_, 1.0, 0.0, MULT, ADD)
+
+        whole_list = slice(0, LIST_COLS)
+        list_halves = [slice(0, LIST_COLS // 2), slice(LIST_COLS // 2, LIST_COLS)]
+
+        def relay_a(r):
+            scores(ring[r % 2], q_tiles[r], keys_w, keys_s, FP8X4, 4)
+            a = leave_psum(f"a{r}", ring[r % 2], nc.vector.tensor_copy if r == 0 else nc.scalar.copy)
+            for piece, cols in enumerate(list_halves if r == 0 else [whole_list]):
+                place(f1[r % WINDOWS], list2, cols, pick(f"a_picked{r}_{piece}", a, list1, cols))
+
+        def make_cc(r):
+            scores(ring[2], q_tiles[r], notes_w, notes_s, FP4X4, 2)
+            return add_in_sbuf(f"cc{r}", ring[2], f1[r % WINDOWS])
+
+        q2_dealt = round_query("q2", q2_raw, round_on_gpsimd)
         cc = []
-        place(f1[0], list2, a_picked[0])
+        relay_a(0)
         for r in range(PACK):
             if r + 1 < PACK:
-                place(f1[(r + 1) % WINDOWS], list2, a_picked[r + 1])
-            scores(ring[r % 2], q_tiles[r], notes_w, notes_s, FP4X4, 2)
-            cc.append(add_scores(f"cc{r}", ring[r % 2], f1[r % WINDOWS]))
+                relay_a(r + 1)
+            cc.append(make_cc(r))
 
         q2_codes, q2_scales = quantize("q2", q2_dealt[:].rearrange("p r s t -> p (r s t)"))
-        cc_picked = []
+
+        def relay_cc(r):
+            place(f2[r % WINDOWS], list4, whole_list, pick(f"cc_picked{r}", cc[r], list3, whole_list))
+
+        def make_dd(r):
+            cols = slice(r * P, (r + 1) * P)
+            scores(ring[r % 2], (q2_codes[:, cols], q2_scales[:, cols]), users_w, users_s, FP4X4, 2)
+            add = add_from_psum if r == PACK - 1 else add_in_sbuf
+            return add(f"dd{r}", ring[r % 2], f2[r % WINDOWS])
+
+        dd = []
+        relay_cc(0)
         for r in range(PACK):
-            values = keep.tile([P, SLOTS], F32, name=f"cc_picked{r}")
-            nc.scalar.activation(values[:], cc[r][:].indirect(list3[:]), COPY)
-            cc_picked.append([(slice(0, LIST_COLS), values)])
+            if r + 1 < PACK:
+                relay_cc(r + 1)
+            dd.append(make_dd(r))
 
         half_slots = SLOTS // 2
         gw = [keep.tile([P, half_slots, PACK], BF16, name=f"gw{h}", align_bytes=64) for h in range(2)]
-        place(f2[0], list4, cc_picked[0])
         for r in range(PACK):
-            if r + 1 < PACK:
-                place(f2[(r + 1) % WINDOWS], list4, cc_picked[r + 1])
-            cols = slice(r * P, (r + 1) * P)
-            scores(ring[r % 2], (q2_codes[:, cols], q2_scales[:, cols]), users_w, users_s, FP4X4, 2)
-            dd = add_scores(f"dd{r}", ring[r % 2], f2[r % WINDOWS])
             factor = row_factor[:, r : r + 1]
-            for h in range(2):
-                g = keep.tile([P, half_slots], F32, name=f"g{r}_{h}")
-                window = dd[:].indirect(list5[:, h * LIST_COLS // 2 : (h + 1) * LIST_COLS // 2])
+            for h, cols in enumerate(list_halves):
                 if r == PACK - 1 and h == 0:
-                    nc.vector.tensor_copy(g[:], window)
+                    g = keep.tile([P, half_slots], F32, name="g_last")
+                    nc.vector.tensor_copy(g[:], dd[r][:].indirect(list5[:, cols]))
                 else:
-                    nc.scalar.activation(g[:], window, COPY)
+                    g = pick(f"g{r}_{h}", dd[r], list5, cols)
                 if r < 2 or h == 1:
                     nc.scalar.activation(gw[h][:, :, r], g[:], COPY, scale=factor)
                 else:

from contextlib import ExitStack

import concourse.mybir as mybir

D, COLS, SLOTS, Q, E = 512, 1024, 512, 512, 256
FLOPS = 2 * D * Q * COLS * 3 + 2 * Q * E * SLOTS

F32 = mybir.dt.float32
BF16 = mybir.dt.bfloat16
I32 = mybir.dt.int32
U32 = mybir.dt.uint32
U16 = mybir.dt.uint16
U8 = mybir.dt.uint8
FP8X4 = mybir.dt.float8_e4m3fn_x4
FP4X4 = mybir.dt.float4_e2m1fn_x4
ADD = mybir.AluOpType.add
MULT = mybir.AluOpType.mult
COPY = mybir.ActivationFunctionType.Copy

P = 128
PACK = 4
BANK = 512
WINDOWS = 3
LIST_COLS = SLOTS // 16


def tile_attend_relaythree_threeq_mixed_kernel(
    tc, query, query2, keys_words, keys_scales, notes_words, notes_scales, users_words, users_scales,
    rowf, mix_words, mix_scales, offs, offs2, offs3, offs4, offs5, out,
):
    nc = tc.nc
    with ExitStack() as ctx:
        keep = ctx.enter_context(tc.tile_pool(name="keep", bufs=1))
        psum = ctx.enter_context(tc.psum_pool(name="psum", bufs=1))
        ring = [[psum.tile([P, BANK], F32, name=f"ring{s}_{h}") for h in range(2)] for s in range(3)]

        def load_list(name, source):
            tile = keep.tile([P, LIST_COLS], U16, name=name)
            nc.sync.dma_start(tile[:], source)
            return tile

        def load_query(name, source):
            halves = []
            for h in range(2):
                raw = keep.tile([P, PACK, Q // 2], F32, name=f"{name}_raw{h}", tag=f"{name}_raw{h}")
                nc.sync.dma_start(
                    out=raw[:],
                    in_=source.rearrange("(p t) q -> p t q", t=PACK)[:, :, h * (Q // 2) : (h + 1) * (Q // 2)],
                )
                halves.append(raw)
            return halves

        def load_words(name, source):
            tile = keep.tile([P, source.shape[1]], U8, name=name, align_bytes=64)
            nc.sync.dma_start(out=tile[:].bitcast(I32), in_=source.bitcast(I32))
            return tile

        def load_scales(name, source, queue):
            tile = keep.tile([P, source.shape[2]], U8, name=name, align_bytes=64)
            for j in range(4):
                queue.dma_start(out=tile[j:P:32, :].bitcast(I32), in_=source[0, j:16:4, :].bitcast(I32))
            return tile

        q_raw = load_query("q", query)
        keys_s = load_scales("keys_s", keys_scales, nc.scalar)
        keys_w = load_words("keys_w", keys_words[0].rearrange("p n t -> p (n t)"))
        list1 = load_list("list1", offs)
        list2 = load_list("list2", offs2)
        notes_w = load_words("notes_w", notes_words[0])
        notes_s = load_scales("notes_s", notes_scales, nc.sync)
        q2_raw = load_query("q2", query2)
        list3 = load_list("list3", offs3)
        list4 = load_list("list4", offs4)
        users_w = load_words("users_w", users_words[0])
        users_s = load_scales("users_s", users_scales, nc.sync)
        list5 = load_list("list5", offs5)
        row_factor = keep.tile([P, PACK], F32)
        nc.sync.dma_start(out=row_factor[:], in_=rowf.rearrange("(p t) o -> p (t o)", t=PACK))
        mix_w = load_words("mix_w", mix_words[0])
        mix_s = load_scales("mix_s", mix_scales, nc.sync)

        f1 = [keep.tile([P, COLS], F32, name=f"f1_{w}") for w in range(WINDOWS)]
        f2 = [keep.tile([P, COLS], F32, name="f2_0")]
        for window in f1 + f2:
            nc.vector.memset(window[:], 0.0)

        def round_query(name, halves, copy):
            dealt = keep.tile([P, PACK, P, PACK], BF16, name=f"{name}_dealt", align_bytes=64)
            for h, raw in enumerate(halves):
                copy(
                    out=dealt[:, :, h * (P // 2) : (h + 1) * (P // 2), :].rearrange("p r s t -> p s r t"),
                    in_=raw[:].rearrange("p t (s r) -> p s r t", r=PACK),
                )
            return dealt

        def quantize(name, values):
            width = values.shape[1] // PACK
            codes = keep.tile([P, width], U32, name=f"{name}_codes", align_bytes=64)
            scales = keep.tile([P, width], U8, name=f"{name}_scales", align_bytes=64)
            nc.vector.quantize_mx(out=codes[:].bitcast(FP8X4), scales=scales[:], in_=values)
            return codes, scales

        def scores(banks, stationary, words, scales, dtype, word_bytes):
            codes, code_scales = stationary
            for half, bank in enumerate(banks):
                nc.tensor.matmul_mx(
                    out=bank[:],
                    lhsT=codes.bitcast(FP8X4),
                    lhsT_scale=code_scales,
                    rhs=words[:, half * BANK * word_bytes : (half + 1) * BANK * word_bytes].bitcast(dtype),
                    rhs_scale=scales[:, half * BANK : (half + 1) * BANK],
                    start=True,
                    stop=True,
                )

        q_dealt = round_query("q", q_raw, nc.vector.tensor_copy)
        q_first = quantize("q_first", q_dealt[:, 0, :, :].rearrange("p s t -> p (s t)"))
        q_rest = quantize("q_rest", q_dealt[:, 1:, :, :].rearrange("p r s t -> p (r s t)"))
        q_tiles = [(q_first[0][:], q_first[1][:])] + [
            (q_rest[0][:, r * P : (r + 1) * P], q_rest[1][:, r * P : (r + 1) * P]) for r in range(PACK - 1)
        ]

        for h in range(2):
            window = keep.tile([P, COLS], F32, name=f"f2_{h + 1}", tag=f"q_raw{h}")
            nc.vector.memset(window[:], 0.0)
            f2.append(window)

        def pick(name, window, entries, cols):
            values = keep.tile([P, 16 * (cols.stop - cols.start)], F32, name=name)
            nc.scalar.activation(values[:], window[:].indirect(entries[:, cols]), COPY)
            return values

        def place(window, places, cols, values):
            nc.vector.tensor_copy(window[:].indirect(places[:, cols]), values[:])

        def leave_psum(name, banks, second_copy):
            whole = keep.tile([P, COLS], F32, name=name)
            nc.scalar.copy(out=whole[:, :BANK], in_=banks[0][:])
            second_copy(out=whole[:, BANK:], in_=banks[1][:])
            return whole

        def add_in_sbuf(name, banks, window):
            total = keep.tile([P, COLS], F32, name=name)
            nc.gpsimd.tensor_tensor(total[:], leave_psum(name + "_term", banks, nc.scalar.copy)[:], window[:], ADD)
            return total

        def add_from_psum(name, banks, window):
            total = keep.tile([P, COLS], F32, name=name)
            for half, bank in enumerate(banks):
                cols = slice(half * BANK, (half + 1) * BANK)
                nc.vector.tensor_tensor(total[:, cols], bank[:], window[:, cols], ADD)
            return total

        def round_on_gpsimd(out, in_):
            nc.gpsimd.tensor_scalar(out, in_, 1.0, 0.0, MULT, ADD)

        whole_list = slice(0, LIST_COLS)
        list_halves = [slice(0, LIST_COLS // 2), slice(LIST_COLS // 2, LIST_COLS)]

        def relay_a(r):
            scores(ring[r % 2], q_tiles[r], keys_w, keys_s, FP8X4, 4)
            a = leave_psum(f"a{r}", ring[r % 2], nc.vector.tensor_copy if r == 0 else nc.scalar.copy)
            for piece, cols in enumerate(list_halves if r == 0 else [whole_list]):
                place(f1[r % WINDOWS], list2, cols, pick(f"a_picked{r}_{piece}", a, list1, cols))

        def make_cc(r):
            scores(ring[2], q_tiles[r], notes_w, notes_s, FP4X4, 2)
            return add_in_sbuf(f"cc{r}", ring[2], f1[r % WINDOWS])

        q2_dealt = round_query("q2", q2_raw, round_on_gpsimd)
        cc = []
        relay_a(0)
        for r in range(PACK):
            if r + 1 < PACK:
                relay_a(r + 1)
            cc.append(make_cc(r))

        q2_codes, q2_scales = quantize("q2", q2_dealt[:].rearrange("p r s t -> p (r s t)"))

        def relay_cc(r):
            place(f2[r % WINDOWS], list4, whole_list, pick(f"cc_picked{r}", cc[r], list3, whole_list))

        def make_dd(r):
            cols = slice(r * P, (r + 1) * P)
            scores(ring[r % 2], (q2_codes[:, cols], q2_scales[:, cols]), users_w, users_s, FP4X4, 2)
            add = add_from_psum if r == PACK - 1 else add_in_sbuf
            return add(f"dd{r}", ring[r % 2], f2[r % WINDOWS])

        dd = []
        relay_cc(0)
        for r in range(PACK):
            if r + 1 < PACK:
                relay_cc(r + 1)
            dd.append(make_dd(r))

        half_slots = SLOTS // 2
        gw = [keep.tile([P, half_slots, PACK], BF16, name=f"gw{h}", align_bytes=64) for h in range(2)]
        for r in range(PACK):
            factor = row_factor[:, r : r + 1]
            for h, cols in enumerate(list_halves):
                if r == PACK - 1 and h == 0:
                    g = keep.tile([P, half_slots], F32, name="g_last")
                    nc.vector.tensor_copy(g[:], dd[r][:].indirect(list5[:, cols]))
                else:
                    g = pick(f"g{r}_{h}", dd[r], list5, cols)
                if r < 2 or h == 1:
                    nc.scalar.activation(gw[h][:, :, r], g[:], COPY, scale=factor)
                else:
                    nc.vector.tensor_scalar_mul(gw[h][:, :, r], g[:], factor)

        for h in range(2):
            codes, scales = quantize(f"gw{h}", gw[h][:].rearrange("p i r -> p (i r)"))
            bank = psum.tile([P, 2, half_slots], F32, name=f"y{h}")
            for e in range(2):
                nc.tensor.matmul_mx(
                    out=bank[:, e, :],
                    lhsT=mix_w[:, e * 2 * P : (e + 1) * 2 * P].bitcast(FP4X4),
                    lhsT_scale=mix_s[:, e * P : (e + 1) * P],
                    rhs=codes[:].bitcast(FP8X4),
                    rhs_scale=scales[:],
                    start=True,
                    stop=True,
                )
            y = keep.tile([P, 2, half_slots], F32, name=f"y_out{h}")
            copy = nc.scalar.copy if h == 0 else nc.vector.tensor_copy
            copy(out=y[:], in_=bank[:])
            queue = nc.scalar if h == 0 else nc.sync
            queue.dma_start(
                out=out.rearrange("(e p) i -> p e i", p=P)[:, :, h * half_slots : (h + 1) * half_slots], in_=y[:]
            )
